import numpy as np
import ml_dtypes


def mxq(x, axis, fmt="e4m3"):
    dtype, down = {"e4m3": (ml_dtypes.float8_e4m3fn, 7), "e5m2": (ml_dtypes.float8_e5m2, 14)}[fmt]
    v = np.moveaxis(np.asarray(x, np.float32).astype(ml_dtypes.bfloat16).astype(np.float64), axis, -1)
    blocks = v.reshape(v.shape[:-1] + (-1, 32))
    amax = np.abs(blocks).max(-1, keepdims=True)
    byte = np.maximum(np.where(amax > 0, np.frexp(amax)[1] - 1 + 127, 0) - down, 1)
    scale = np.exp2(byte - 127.0)
    codes = (blocks / scale).astype(np.float32).astype(dtype).astype(np.float64)
    return np.moveaxis((codes * scale).reshape(v.shape), -1, axis)


WIDE = False


def mx_kscale(k):
    if not WIDE:
        return np.ones(k)
    levels = np.array([10, -10, 5, -5, 0])
    if k % 512:
        return np.exp2(np.random.permutation(np.resize(levels, k // 32))).repeat(32)
    a = np.empty((k // 512, 16))
    for p in range(k // 512):
        a[p, :8] = np.random.permutation(np.resize(levels, 8))
        for g in range(8):
            far = levels[np.abs(levels - a[p, g]) >= 10]
            a[p, g + 8] = far[np.random.randint(len(far))]
    return np.exp2(a.ravel()).repeat(32)


def f64(x):
    return np.asarray(x).astype(np.float64)


def striped(idx):
    return np.tile(idx.reshape(-1, 16).T, (8, 1)).astype(np.uint16)


def unstriped(offs):
    return offs[:16].T.reshape(-1).astype(np.int64)


E2M1 = np.array([0.0, 0.5, 1.0, 1.5, 2.0, 3.0, 4.0, 6.0, -0.0, -0.5, -1.0, -1.5, -2.0, -3.0, -4.0, -6.0])


def pack_weight(w, fmt):
    k, n = w.shape
    w = f64(np.asarray(w, np.float32).astype(ml_dtypes.bfloat16)).reshape(k // 32, 32, n)
    amax = np.abs(w).max(1)
    if fmt == "e4m3":
        byte = np.frexp(amax)[1] - 1 + 127 - 7
    else:
        mant, ex = np.frexp(amax / 6.0)
        byte = np.where(mant > 0.5, ex, ex - 1) + 127
    byte = np.clip(np.where(amax > 0, byte, 1), 1, 254)
    scaled = (w * np.exp2(127.0 - byte)[:, None, :]).reshape(k, n).astype(np.float32)
    by_word = np.ascontiguousarray(scaled.reshape(k // 512, 128, 4, n).transpose(0, 1, 3, 2))
    if fmt == "e4m3":
        words = by_word.astype(ml_dtypes.float8_e4m3fn).view(np.uint8)
    else:
        c = by_word.astype(ml_dtypes.float4_e2m1fn).view(np.uint8) & 0xF
        words = (c[..., 0::2] | (c[..., 1::2] << 4)).reshape(k // 512, 128, 2 * n)
    return np.ascontiguousarray(words), np.ascontiguousarray(byte.astype(np.uint8).reshape(k // 512, 16, n))


def unpack_weight(words, scales, fmt):
    g, _, n = scales.shape
    words = np.ascontiguousarray(words).reshape(g, 128, n, -1)
    if fmt == "e4m3":
        vals = words.view(ml_dtypes.float8_e4m3fn).astype(np.float64)
    else:
        nib = np.empty((g, 128, n, 4), np.uint8)
        nib[..., 0::2] = words & 0xF
        nib[..., 1::2] = words >> 4
        vals = E2M1[nib]
    vals = vals * np.repeat(np.exp2(scales.astype(np.float64) - 127.0), 8, axis=1)[..., None]
    return vals.transpose(0, 1, 3, 2).reshape(g * 512, n)


K, T, E, C, N = 512, 768, 6, 128, 1024
M = 512


def by_expert(wq, xq):
    return np.concatenate([wq[e].T @ xq[:, e * C:(e + 1) * C] for e in range(E)], axis=1)


def setup_inputs():
    n = np.random.standard_normal
    s = mx_kscale(K)[:, None]
    v = mx_kscale(N)
    w = [pack_weight(m, "e2m1") for m in n((E, K, N)) / np.sqrt(K) / s[None] * v[None, None, :]]
    return {
        "xT": (n((K, T)) * s).astype(np.float32),
        "w_words": np.stack([m[0] for m in w]),
        "w_scales": np.stack([m[1] for m in w]),
        "wp": (n((N, M)) / np.sqrt(N) / v[:, None]).astype(np.float32),
        "gate": np.tile(np.random.uniform(0.2, 1.0, E * C), (N, 1)).astype(np.float32),
        "offs": striped(np.random.permutation(T)[:E * C]),
    }


def reference(xT, w_words, w_scales, wp, gate, offs):
    idx = unstriped(offs)
    w = np.stack([unpack_weight(w_words[e], w_scales[e], "e2m1") for e in range(E)])
    xq = mxq(f64(xT)[:, idx], 0, "e4m3")
    y = by_expert(w, xq)
    c = np.zeros((N, T))
    c[:, idx] = f64(gate) * y
    return mxq(f64(wp), 0, "e4m3").T @ mxq(c, 0, "e4m3")

@@ -1,0 +1,238 @@
+from contextlib import ExitStack
+
+import concourse.mybir as mybir
+from concourse.masks import make_identity
+
+K, T, E, C, N, M = 512, 768, 6, 128, 1024, 512
+P = 128
+PACK = 4
+PASSES = N // 512
+F_TILES = M // P
+
+FLOPS = 2 * K * N * E * C + 2 * N * M * T
+BYTES = 4 * K * T + E * K * N // 2 + E * (K // 32) * N + 4 * N * M + 4 * E * C + 2 * E * C + 4 * M * T
+
+F32 = mybir.dt.float32
+BF16 = mybir.dt.bfloat16
+I32 = mybir.dt.int32
+U32 = mybir.dt.uint32
+U16 = mybir.dt.uint16
+U8 = mybir.dt.uint8
+FP8X4 = mybir.dt.float8_e4m3fn_x4
+FP4X4 = mybir.dt.float4_e2m1fn_x4
+COPY = mybir.ActivationFunctionType.Copy
+
+
+def interleave(copy, dst, src, a, b):
+    copy(
+        out=dst[:, PACK * a : PACK * b].rearrange("p (c i j) -> p c j i", i=4, j=PACK),
+        in_=src[:, :, a:b].rearrange("p j (c i) -> p c j i", i=4),
+    )
+
+
+def tile_moe_nxt_lin_none_kernel(tc, xT, w_words, w_scales, wp, gate, offs, out):
+    nc = tc.nc
+    with ExitStack() as ctx:
+        keep = ctx.enter_context(tc.tile_pool(name="keep", bufs=1))
+        ring = ctx.enter_context(tc.tile_pool(name="ring", bufs=3))
+        psum_y = ctx.enter_context(tc.psum_pool(name="psum_y", bufs=4))
+        psum_t = ctx.enter_context(tc.psum_pool(name="psum_t", bufs=2))
+        psum_o = ctx.enter_context(tc.psum_pool(name="psum_o", bufs=2))
+
+        offsets = keep.tile([P, E * C // 16], U16, name="offsets")
+        gate_cols = keep.tile([P, E], F32, name="gate_cols")
+        ident = keep.tile([P, P], F32, name="ident")
+        x_codes = keep.tile([P, T], U32, name="x_codes", align_bytes=64)
+        x_scales = keep.tile([P, T], U8, name="x_scales", align_bytes=64)
+        s_codes = keep.tile([P, E * C], U32, name="s_codes", align_bytes=64)
+        s_scales = keep.tile([P, E * C], U8, name="s_scales", align_bytes=64)
+        w_codes = keep.tile([P, E, 2 * N], U8, name="w_codes", align_bytes=64)
+        w_planes = keep.tile([P, E, N], U8, name="w_planes", align_bytes=64)
+
+        nc.vector.memset(w_planes[:].rearrange("p e n -> p (e n)").bitcast(I32), 0)
+        nc.gpsimd.memset(x_scales[:], 0)
+        make_identity(nc, ident[:])
+
+        x_view = xT.rearrange("(p j) t -> p j t", j=PACK)
+        x_cuts = ((0, 512), (512, T))
+        x_raw = []
+        for a, b in x_cuts:
+            raw = keep.tile([P, PACK, b - a], F32, name=f"x_raw{a}")
+            nc.sync.dma_start(out=raw[:], in_=x_view[:, :, a:b])
+            x_raw.append(raw)
+        nc.sync.dma_start(offsets[:], offs)
+        with nc.allow_non_contiguous_dma(reason="one gate value a slot, 768 in all"):
+            nc.scalar.dma_start(out=gate_cols[:], in_=gate[0:1, :].rearrange("o (e p) -> p (o e)", p=P))
+
+        def load_w(a, b):
+            for e in range(a, b):
+                nc.sync.dma_start(out=w_codes[:, e, :].bitcast(I32), in_=w_words[e, 0].bitcast(I32))
+
+        wp_view = wp.rearrange("(g p j) f -> g p j f", p=P, j=PACK)
+        wp_raw = {}
+
+        def load_wp(half):
+            for g in range(PASSES):
+                raw = keep.tile([P, PACK, M // 2], F32, name=f"wp_raw{half}{g}")
+                nc.sync.dma_start(out=raw[:], in_=wp_view[g, :, :, half * (M // 2) : (half + 1) * (M // 2)])
+                wp_raw[half, g] = raw
+
+        load_w(0, 1)
+        scale_rows = w_scales.bitcast(I32).rearrange("e a (q r) n -> r q (e a) n", r=4)
+        for r in range(4):
+            nc.sync.dma_start(out=w_planes[r:P:32, :, :].bitcast(I32), in_=scale_rows[r])
+        load_wp(0)
+        load_w(1, 3)
+        load_wp(1)
+        load_w(3, E)
+
+        x_group = keep.tile([P, PACK * T], BF16, name="x_group", align_bytes=64)
+        for (a, b), raw in zip(x_cuts, x_raw):
+            width = b - a
+            dst = x_group[:, PACK * a : PACK * b]
+            cut = width // 2
+            interleave(nc.scalar.copy, dst, raw, 0, cut)
+            interleave(nc.vector.tensor_copy, dst, raw, cut, width)
+            nc.vector.quantize_mx(out=x_codes[:, a:b].bitcast(FP8X4), scales=x_scales[:, a:b], in_=dst)
+
+        def gather(a, b):
+            at = offsets[:, a * C // 16 : b * C // 16]
+            nc.vector.tensor_copy(s_codes[:, a * C : b * C], x_codes[:].indirect(at))
+            nc.vector.tensor_copy(s_scales[:, a * C : b * C], x_scales[:].indirect(at))
+
+        grouped = {}
+        c_quant = {}
+
+        def experts_product(e):
+            c_rows = ring.tile([P, N], BF16, name="c_rows", align_bytes=64)
+            for g in range(PASSES):
+                y = psum_y.tile([P, 512], F32, name="y")
+                nc.tensor.matmul_mx(
+                    out=y[:],
+                    lhsT=s_codes[:, e * C : (e + 1) * C].bitcast(FP8X4),
+                    lhsT_scale=s_scales[:, e * C : (e + 1) * C],
+                    rhs=w_codes[:, e, 1024 * g : 1024 * (g + 1)].bitcast(FP4X4),
+                    rhs_scale=w_planes[:, e, 512 * g : 512 * (g + 1)],
+                    start=True,
+                    stop=True,
+                )
+                nc.scalar.activation(
+                    out=c_rows[:, 512 * g : 512 * (g + 1)].rearrange("s (u p i) -> s u p i", u=2, i=2),
+                    in_=y[:].rearrange("s (p u i) -> s u p i", u=2, i=2),
+                    func=COPY,
+                    scale=gate_cols[:, e : e + 1],
+                )
+            turned = psum_t.tile([P, PASSES, 2, C], F32, name="turned")
+            words = c_rows[:].bitcast(F32)
+            for g in range(PASSES):
+                for u in range(2):
+                    at = 256 * g + 128 * u
+                    nc.tensor.transpose(turned[:, g, u, :], words[:, at : at + 128], ident[:])
+            c_group = ring.tile([P, PASSES * C * PACK], BF16, name="c_group", align_bytes=64)
+            nc.scalar.copy(
+                out=c_group[:].bitcast(F32).rearrange("p (g s u) -> p g s u", g=PASSES, u=2),
+                in_=turned[:].rearrange("p g u s -> p g s u"),
+            )
+            grouped[e] = c_group
+
+        def quantise_c(e):
+            c_codes = ring.tile([P, PASSES, C], U32, name="c_codes", align_bytes=64)
+            c_scales = ring.tile([P, PASSES, C], U8, name="c_scales", align_bytes=64)
+            nc.vector.quantize_mx(
+                out=c_codes[:].rearrange("p g s -> p (g s)").bitcast(FP8X4),
+                scales=c_scales[:].rearrange("p g s -> p (g s)"),
+                in_=grouped[e][:],
+            )
+            c_quant[e] = (c_codes, c_scales)
+
+        wp_codes, wp_scales, wp_group = {}, {}, {}
+
+        def prepare_wp(half):
+            width = M // 2
+            group = keep.tile([P, PASSES * width * PACK], BF16, name=f"wp_group{half}", align_bytes=64)
+            for g in range(PASSES):
+                dst = group[:, PACK * width * g : PACK * width * (g + 1)]
+                if g == 0:
+                    interleave(nc.scalar.copy, dst, wp_raw[half, g], 0, width)
+                else:
+                    interleave(nc.vector.tensor_copy, dst, wp_raw[half, g], 0, width)
+            wp_group[half] = group
+
+        def quantise_wp(half):
+            width = M // 2
+            codes = keep.tile([P, PASSES, width], U32, name=f"wp_codes{half}", align_bytes=64)
+            scales = keep.tile([P, PASSES, width], U8, name=f"wp_scales{half}", align_bytes=64)
+            nc.vector.quantize_mx(
+                out=codes[:].rearrange("p g f -> p (g f)").bitcast(FP8X4),
+                scales=scales[:].rearrange("p g f -> p (g f)"),
+                in_=wp_group[half][:],
+            )
+            wp_codes[half], wp_scales[half] = codes, scales
+
+        windows = [keep.tile([P, T], F32, name=f"window{f}") for f in range(F_TILES)]
+
+        def next_projection(e, f_tiles, landed, col):
+            o = psum_o.tile([P, F_TILES * C], F32, name="o")
+            c_codes, c_scales = c_quant[e]
+            for i, f in enumerate(f_tiles):
+                half, at = f // 2, (f % 2) * P
+                for g in range(PASSES):
+                    nc.tensor.matmul_mx(
+                        out=o[:, i * C : (i + 1) * C],
+                        lhsT=wp_codes[half][:, g, at : at + P].bitcast(FP8X4),
+                        lhsT_scale=wp_scales[half][:, g, at : at + P],
+                        rhs=c_codes[:, g, :].bitcast(FP8X4),
+                        rhs_scale=c_scales[:, g, :],
+                        start=(g == 0),
+                        stop=(g == PASSES - 1),
+                    )
+            lo, hi = f_tiles[0], f_tiles[-1] + 1
+            nc.scalar.copy(
+                out=landed[:, lo:hi, col : col + C],
+                in_=o[:, : len(f_tiles) * C].rearrange("p (f s) -> p f s", s=C),
+            )
+
+        def scatter(landed, a, b, f):
+            nc.vector.tensor_copy(windows[f][:].indirect(offsets[:, a * C // 16 : b * C // 16]), landed[:, f, :])
+
+        gather(0, 1)
+        experts_product(0)
+        gather(1, 3)
+        experts_product(1)
+        quantise_c(0)
+        prepare_wp(0)
+        gather(3, E)
+        quantise_wp(0)
+        landed0 = keep.tile([P, F_TILES, C], F32, name="landed0")
+        next_projection(0, (0, 1), landed0, 0)
+        quantise_c(1)
+        scatter(landed0, 0, 1, 0)
+        scatter(landed0, 0, 1, 1)
+        experts_product(2)
+        prepare_wp(1)
+        quantise_wp(1)
+        quantise_c(2)
+        next_projection(0, (2, 3), landed0, 0)
+        scatter(landed0, 0, 1, 2)
+        scatter(landed0, 0, 1, 3)
+        landed1 = keep.tile([P, F_TILES, C], F32, name="landed1")
+        next_projection(1, (0, 1, 2, 3), landed1, 0)
+        experts_product(3)
+        quantise_c(3)
+        for f in range(F_TILES):
+            scatter(landed1, 1, 2, f)
+        landed2 = keep.tile([P, F_TILES, 2 * C], F32, name="landed2")
+        next_projection(2, (0, 1, 2, 3), landed2, 0)
+        experts_product(4)
+        next_projection(3, (0, 1, 2, 3), landed2, C)
+        quantise_c(4)
+        experts_product(5)
+        quantise_c(5)
+        for f in range(F_TILES):
+            scatter(landed2, 2, 4, f)
+        landed4 = keep.tile([P, F_TILES, 2 * C], F32, name="landed4")
+        next_projection(4, (0, 1, 2, 3), landed4, 0)
+        next_projection(5, (0, 1, 2, 3), landed4, C)
+        for f in range(F_TILES):
+            scatter(landed4, 4, 6, f)
+            nc.sync.dma_start(out=out[f * P : (f + 1) * P, :], in_=windows[f][:])

@@ -21,6 +21,7 @@ U8 = mybir.dt.uint8
 FP8X4 = mybir.dt.float8_e4m3fn_x4
 FP4X4 = mybir.dt.float4_e2m1fn_x4
 COPY = mybir.ActivationFunctionType.Copy
+MULT = mybir.AluOpType.mult
 
 
 def interleave(copy, dst, src, a, b):
@@ -41,6 +42,7 @@ def tile_moe_nxt_lin_none_kernel(tc, xT, w_words, w_scales, wp, gate, offs, out)
 
         offsets = keep.tile([P, E * C // 16], U16, name="offsets")
         gate_cols = keep.tile([P, E], F32, name="gate_cols")
+        gate_rows = keep.tile([P, P], F32, name="gate_rows")
         ident = keep.tile([P, P], F32, name="ident")
         x_codes = keep.tile([P, T], U32, name="x_codes", align_bytes=64)
         x_scales = keep.tile([P, T], U8, name="x_scales", align_bytes=64)
@@ -51,39 +53,39 @@ def tile_moe_nxt_lin_none_kernel(tc, xT, w_words, w_scales, wp, gate, offs, out)
 
         nc.vector.memset(w_planes[:].rearrange("p e n -> p (e n)").bitcast(I32), 0)
         nc.gpsimd.memset(x_scales[:], 0)
+        nc.gpsimd.memset(gate_rows[:], 0.0)
         make_identity(nc, ident[:])
 
         x_view = xT.rearrange("(p j) t -> p j t", j=PACK)
-        x_cuts = ((0, 512), (512, T))
+        x_cuts = ((0, 512), (512, 640), (640, T))
         x_raw = []
         for a, b in x_cuts:
             raw = keep.tile([P, PACK, b - a], F32, name=f"x_raw{a}")
             nc.sync.dma_start(out=raw[:], in_=x_view[:, :, a:b])
             x_raw.append(raw)
         nc.sync.dma_start(offsets[:], offs)
-        with nc.allow_non_contiguous_dma(reason="one gate value a slot, 768 in all"):
-            nc.scalar.dma_start(out=gate_cols[:], in_=gate[0:1, :].rearrange("o (e p) -> p (o e)", p=P))
+        nc.sync.dma_start(out=gate_rows[0:E, :], in_=gate[0:1, :].rearrange("o (e p) -> (o e) p", p=P))
 
         def load_w(a, b):
-            for e in range(a, b):
-                nc.sync.dma_start(out=w_codes[:, e, :].bitcast(I32), in_=w_words[e, 0].bitcast(I32))
+            nc.sync.dma_start(out=w_codes[:, a:b, :].bitcast(I32), in_=w_words[a:b, 0].rearrange("e p n -> p e n").bitcast(I32))
 
         wp_view = wp.rearrange("(g p j) f -> g p j f", p=P, j=PACK)
         wp_raw = {}
 
-        def load_wp(half):
-            for g in range(PASSES):
-                raw = keep.tile([P, PACK, M // 2], F32, name=f"wp_raw{half}{g}")
-                nc.sync.dma_start(out=raw[:], in_=wp_view[g, :, :, half * (M // 2) : (half + 1) * (M // 2)])
-                wp_raw[half, g] = raw
+        def load_wp(half, g):
+            raw = keep.tile([P, PACK, M // 2], F32, name=f"wp_raw{half}{g}")
+            nc.sync.dma_start(out=raw[:], in_=wp_view[g, :, :, half * (M // 2) : (half + 1) * (M // 2)])
+            wp_raw[half, g] = raw
 
+        load_wp(0, 0)
         load_w(0, 1)
         scale_rows = w_scales.bitcast(I32).rearrange("e a (q r) n -> r q (e a) n", r=4)
         for r in range(4):
             nc.sync.dma_start(out=w_planes[r:P:32, :, :].bitcast(I32), in_=scale_rows[r])
-        load_wp(0)
+        load_wp(0, 1)
         load_w(1, 3)
-        load_wp(1)
+        load_wp(1, 0)
+        load_wp(1, 1)
         load_w(3, E)
 
         x_group = keep.tile([P, PACK * T], BF16, name="x_group", align_bytes=64)
@@ -100,11 +102,18 @@ def tile_moe_nxt_lin_none_kernel(tc, xT, w_words, w_scales, wp, gate, offs, out)
             nc.vector.tensor_copy(s_codes[:, a * C : b * C], x_codes[:].indirect(at))
             nc.vector.tensor_copy(s_scales[:, a * C : b * C], x_scales[:].indirect(at))
 
-        grouped = {}
-        c_quant = {}
+        def gate_times(e, g, y, c_rows, on_vector):
+            dst = c_rows[:, 512 * g : 512 * (g + 1)].rearrange("s (u p i) -> s u p i", u=2, i=2)
+            src = y[:].rearrange("s (p u i) -> s u p i", u=2, i=2)
+            if on_vector:
+                nc.vector.tensor_scalar(dst, src, gate_cols[:, e : e + 1], None, MULT)
+            else:
+                nc.scalar.activation(out=dst, in_=src, func=COPY, scale=gate_cols[:, e : e + 1])
 
-        def experts_product(e):
-            c_rows = ring.tile([P, N], BF16, name="c_rows", align_bytes=64)
+        ys = {}
+
+        def product(e):
+            ys[e] = []
             for g in range(PASSES):
                 y = psum_y.tile([P, 512], F32, name="y")
                 nc.tensor.matmul_mx(
@@ -116,123 +125,147 @@ def tile_moe_nxt_lin_none_kernel(tc, xT, w_words, w_scales, wp, gate, offs, out)
                     start=True,
                     stop=True,
                 )
-                nc.scalar.activation(
-                    out=c_rows[:, 512 * g : 512 * (g + 1)].rearrange("s (u p i) -> s u p i", u=2, i=2),
-                    in_=y[:].rearrange("s (p u i) -> s u p i", u=2, i=2),
-                    func=COPY,
-                    scale=gate_cols[:, e : e + 1],
-                )
+                ys[e].append(y)
+
+        groups = {}
+
+        rows, turned_of, groups, c_quant, sums, landed = {}, {}, {}, {}, {}, {}
+
+        def gated_rows(e, g, on_vector=False):
+            if g == 0:
+                rows[e] = ring.tile([P, N], BF16, name="c_rows", align_bytes=64)
+            gate_times(e, g, ys[e][g], rows[e], on_vector)
+
+        def turn(e):
             turned = psum_t.tile([P, PASSES, 2, C], F32, name="turned")
-            words = c_rows[:].bitcast(F32)
+            words = rows[e][:].bitcast(F32)
             for g in range(PASSES):
                 for u in range(2):
                     at = 256 * g + 128 * u
                     nc.tensor.transpose(turned[:, g, u, :], words[:, at : at + 128], ident[:])
-            c_group = ring.tile([P, PASSES * C * PACK], BF16, name="c_group", align_bytes=64)
-            nc.scalar.copy(
-                out=c_group[:].bitcast(F32).rearrange("p (g s u) -> p g s u", g=PASSES, u=2),
-                in_=turned[:].rearrange("p g u s -> p g s u"),
-            )
-            grouped[e] = c_group
+            turned_of[e] = turned
 
-        def quantise_c(e):
-            c_codes = ring.tile([P, PASSES, C], U32, name="c_codes", align_bytes=64)
-            c_scales = ring.tile([P, PASSES, C], U8, name="c_scales", align_bytes=64)
+        def group_c(unit, e):
+            width = len(unit) * C
+            if e == unit[0]:
+                groups[unit] = keep.tile([P, PASSES, width, PACK], BF16, name=f"c_group{e}", align_bytes=64)
+            words = groups[unit][:].rearrange("p g s j -> p (g s j)").bitcast(F32).rearrange("p (g s u) -> p g s u", g=PASSES, u=2)
+            at = (e - unit[0]) * C
+            nc.scalar.copy(out=words[:, :, at : at + C, :], in_=turned_of[e][:].rearrange("p g u s -> p g s u"))
+
+        def quantise_c(unit):
+            width = len(unit) * C
+            codes = keep.tile([P, PASSES, width], U32, name=f"c_codes{unit[0]}", align_bytes=64)
+            scales = keep.tile([P, PASSES, width], U8, name=f"c_scales{unit[0]}", align_bytes=64)
             nc.vector.quantize_mx(
-                out=c_codes[:].rearrange("p g s -> p (g s)").bitcast(FP8X4),
-                scales=c_scales[:].rearrange("p g s -> p (g s)"),
-                in_=grouped[e][:],
+                out=codes[:].rearrange("p g s -> p (g s)").bitcast(FP8X4),
+                scales=scales[:].rearrange("p g s -> p (g s)"),
+                in_=groups[unit][:].rearrange("p g s j -> p (g s j)"),
             )
-            c_quant[e] = (c_codes, c_scales)
+            c_quant[unit] = (codes, scales)
 
-        wp_codes, wp_scales, wp_group = {}, {}, {}
+        half_width = M // 2
+        wp_codes, wp_scales, wp_group = [], [], []
+        for half in range(2):
+            wp_group.append(keep.tile([P, PASSES * half_width * PACK], BF16, name=f"wp_group{half}", align_bytes=64))
+            wp_codes.append(keep.tile([P, PASSES, half_width], U32, name=f"wp_codes{half}", align_bytes=64))
+            wp_scales.append(keep.tile([P, PASSES, half_width], U8, name=f"wp_scales{half}", align_bytes=64))
 
-        def prepare_wp(half):
-            width = M // 2
-            group = keep.tile([P, PASSES * width * PACK], BF16, name=f"wp_group{half}", align_bytes=64)
-            for g in range(PASSES):
-                dst = group[:, PACK * width * g : PACK * width * (g + 1)]
-                if g == 0:
-                    interleave(nc.scalar.copy, dst, wp_raw[half, g], 0, width)
-                else:
-                    interleave(nc.vector.tensor_copy, dst, wp_raw[half, g], 0, width)
-            wp_group[half] = group
+        def pool_copy(out, in_):
+            nc.gpsimd.tensor_scalar(out, in_, 1.0, 0.0, MULT, mybir.AluOpType.add)
+
+        def group_wp(half, g, copy):
+            dst = wp_group[half][:, PACK * half_width * g : PACK * half_width * (g + 1)]
+            interleave(copy, dst, wp_raw[half, g], 0, half_width)
 
         def quantise_wp(half):
-            width = M // 2
-            codes = keep.tile([P, PASSES, width], U32, name=f"wp_codes{half}", align_bytes=64)
-            scales = keep.tile([P, PASSES, width], U8, name=f"wp_scales{half}", align_bytes=64)
             nc.vector.quantize_mx(
-                out=codes[:].rearrange("p g f -> p (g f)").bitcast(FP8X4),
-                scales=scales[:].rearrange("p g f -> p (g f)"),
+                out=wp_codes[half][:].rearrange("p g f -> p (g f)").bitcast(FP8X4),
+                scales=wp_scales[half][:].rearrange("p g f -> p (g f)"),
                 in_=wp_group[half][:],
             )
-            wp_codes[half], wp_scales[half] = codes, scales
 
         windows = [keep.tile([P, T], F32, name=f"window{f}") for f in range(F_TILES)]
 
-        def next_projection(e, f_tiles, landed, col):
-            o = psum_o.tile([P, F_TILES * C], F32, name="o")
-            c_codes, c_scales = c_quant[e]
+        def next_projection(unit, f_tiles):
+            width = len(unit) * C
+            o = psum_o.tile([P, 512], F32, name="o")
+            codes, scales = c_quant[unit]
             for i, f in enumerate(f_tiles):
                 half, at = f // 2, (f % 2) * P
                 for g in range(PASSES):
                     nc.tensor.matmul_mx(
-                        out=o[:, i * C : (i + 1) * C],
+                        out=o[:, i * width : (i + 1) * width],
                         lhsT=wp_codes[half][:, g, at : at + P].bitcast(FP8X4),
                         lhsT_scale=wp_scales[half][:, g, at : at + P],
-                        rhs=c_codes[:, g, :].bitcast(FP8X4),
-                        rhs_scale=c_scales[:, g, :],
+                        rhs=codes[:, g, :].bitcast(FP8X4),
+                        rhs_scale=scales[:, g, :],
                         start=(g == 0),
                         stop=(g == PASSES - 1),
                     )
-            lo, hi = f_tiles[0], f_tiles[-1] + 1
-            nc.scalar.copy(
-                out=landed[:, lo:hi, col : col + C],
-                in_=o[:, : len(f_tiles) * C].rearrange("p (f s) -> p f s", s=C),
-            )
+            sums[unit, f_tiles] = o
 
-        def scatter(landed, a, b, f):
-            nc.vector.tensor_copy(windows[f][:].indirect(offsets[:, a * C // 16 : b * C // 16]), landed[:, f, :])
+        def land(unit, f_tiles):
+            width = len(unit) * C
+            tile = keep.tile([P, len(f_tiles), width], F32, name=f"landed{unit[0]}{f_tiles[0]}")
+            nc.scalar.copy(
+                out=tile[:].rearrange("p f s -> p (f s)"), in_=sums[unit, f_tiles][:, : len(f_tiles) * width]
+            )
+            for i, f in enumerate(f_tiles):
+                landed[unit, f] = tile[:, i, :]
+
+        def scatter(unit, f):
+            a, b = unit[0], unit[-1] + 1
+            nc.vector.tensor_copy(windows[f][:].indirect(offsets[:, a * C // 16 : b * C // 16]), landed[unit, f])
+
+        low, high = (0, 1), (2, 3)
+        first, second, third, fourth = (0,), (1,), (2, 3), (4, 5)
 
         gather(0, 1)
-        experts_product(0)
-        gather(1, 3)
-        experts_product(1)
-        quantise_c(0)
-        prepare_wp(0)
-        gather(3, E)
+        turned = psum_t.tile([P, PASSES, 2, C], F32, name="turned")
+        nc.tensor.transpose(turned[:, 0, 0, :], gate_rows[:], ident[:])
+        nc.vector.tensor_copy(out=gate_cols[:], in_=turned[:, 0, 0, 0:E])
+        product(0)
+        group_wp(0, 0, nc.scalar.copy)
+        gated_rows(0, 0)
+        gated_rows(0, 1, True)
+        turn(0)
+        group_c(first, 0)
+        group_wp(0, 1, nc.scalar.copy)
+        quantise_c(first)
         quantise_wp(0)
-        landed0 = keep.tile([P, F_TILES, C], F32, name="landed0")
-        next_projection(0, (0, 1), landed0, 0)
-        quantise_c(1)
-        scatter(landed0, 0, 1, 0)
-        scatter(landed0, 0, 1, 1)
-        experts_product(2)
-        prepare_wp(1)
+        next_projection(first, low)
+        land(first, low)
+        gather(1, 3)
+        product(1)
+        gated_rows(1, 0)
+        gated_rows(1, 1)
+        turn(1)
+        group_c(second, 1)
+        quantise_c(second)
+        next_projection(second, low)
+        land(second, low)
+        group_wp(1, 0, pool_copy)
+        group_wp(1, 1, nc.vector.tensor_copy)
         quantise_wp(1)
-        quantise_c(2)
-        next_projection(0, (2, 3), landed0, 0)
-        scatter(landed0, 0, 1, 2)
-        scatter(landed0, 0, 1, 3)
-        landed1 = keep.tile([P, F_TILES, C], F32, name="landed1")
-        next_projection(1, (0, 1, 2, 3), landed1, 0)
-        experts_product(3)
-        quantise_c(3)
-        for f in range(F_TILES):
-            scatter(landed1, 1, 2, f)
-        landed2 = keep.tile([P, F_TILES, 2 * C], F32, name="landed2")
-        next_projection(2, (0, 1, 2, 3), landed2, 0)
-        experts_product(4)
-        next_projection(3, (0, 1, 2, 3), landed2, C)
-        quantise_c(4)
-        experts_product(5)
-        quantise_c(5)
-        for f in range(F_TILES):
-            scatter(landed2, 2, 4, f)
-        landed4 = keep.tile([P, F_TILES, 2 * C], F32, name="landed4")
-        next_projection(4, (0, 1, 2, 3), landed4, 0)
-        next_projection(5, (0, 1, 2, 3), landed4, C)
-        for f in range(F_TILES):
-            scatter(landed4, 4, 6, f)
+        gather(3, E)
+        for unit in (first, second):
+            next_projection(unit, high)
+            land(unit, high)
+        for unit in (third, fourth):
+            for e in unit:
+                product(e)
+                gated_rows(e, 0)
+                gated_rows(e, 1)
+                turn(e)
+                group_c(unit, e)
+            quantise_c(unit)
+            for half in (low, high):
+                next_projection(unit, half)
+                land(unit, half)
+        for unit in (first, second, third):
+            for f in low + high:
+                scatter(unit, f)
+        for f in low + high:
+            scatter(fourth, f)
             nc.sync.dma_start(out=out[f * P : (f + 1) * P, :], in_=windows[f][:])

@@ -57,7 +57,7 @@ def tile_moe_nxt_lin_none_kernel(tc, xT, w_words, w_scales, wp, gate, offs, out)
         make_identity(nc, ident[:])
 
         x_view = xT.rearrange("(p j) t -> p j t", j=PACK)
-        x_cuts = ((0, 512), (512, 640), (640, T))
+        x_cuts = ((0, 256), (256, 512), (512, T))
         x_raw = []
         for a, b in x_cuts:
             raw = keep.tile([P, PACK, b - a], F32, name=f"x_raw{a}")
@@ -92,7 +92,7 @@ def tile_moe_nxt_lin_none_kernel(tc, xT, w_words, w_scales, wp, gate, offs, out)
         for (a, b), raw in zip(x_cuts, x_raw):
             width = b - a
             dst = x_group[:, PACK * a : PACK * b]
-            cut = width // 2
+            cut = 96
             interleave(nc.scalar.copy, dst, raw, 0, cut)
             interleave(nc.vector.tensor_copy, dst, raw, cut, width)
             nc.vector.quantize_mx(out=x_codes[:, a:b].bitcast(FP8X4), scales=x_scales[:, a:b], in_=dst)
@@ -148,7 +148,7 @@ def tile_moe_nxt_lin_none_kernel(tc, xT, w_words, w_scales, wp, gate, offs, out)
         def group_c(unit, e):
             width = len(unit) * C
             if e == unit[0]:
-                groups[unit] = keep.tile([P, PASSES, width, PACK], BF16, name=f"c_group{e}", align_bytes=64)
+                groups[unit] = keep.tile([P, PASSES, width, PACK], BF16, name=f"c_group{e}", tag=f"swap{e}", align_bytes=64)
             words = groups[unit][:].rearrange("p g s j -> p (g s j)").bitcast(F32).rearrange("p (g s u) -> p g s u", g=PASSES, u=2)
             at = (e - unit[0]) * C
             nc.scalar.copy(out=words[:, :, at : at + C, :], in_=turned_of[e][:].rearrange("p g u s -> p g s u"))
@@ -205,9 +205,11 @@ def tile_moe_nxt_lin_none_kernel(tc, xT, w_words, w_scales, wp, gate, offs, out)
                     )
             sums[unit, f_tiles] = o
 
-        def land(unit, f_tiles):
+        def land(unit, f_tiles, after=None):
             width = len(unit) * C
-            tile = keep.tile([P, len(f_tiles), width], F32, name=f"landed{unit[0]}{f_tiles[0]}")
+            label = f"landed{unit[0]}{f_tiles[0]}"
+            tag = f"swap{after[0]}" if after else label
+            tile = keep.tile([P, len(f_tiles), width], F32, name=label, tag=tag, align_bytes=64)
             nc.scalar.copy(
                 out=tile[:].rearrange("p f s -> p (f s)"), in_=sums[unit, f_tiles][:, : len(f_tiles) * width]
             )
@@ -219,7 +221,7 @@ def tile_moe_nxt_lin_none_kernel(tc, xT, w_words, w_scales, wp, gate, offs, out)
             nc.vector.tensor_copy(windows[f][:].indirect(offsets[:, a * C // 16 : b * C // 16]), landed[unit, f])
 
         low, high = (0, 1), (2, 3)
-        first, second, third, fourth = (0,), (1,), (2, 3), (4, 5)
+        units = ((0,), (1,), (2,), (3, 4), (5,))
 
         gather(0, 1)
         turned = psum_t.tile([P, PASSES, 2, C], F32, name="turned")
@@ -230,42 +232,38 @@ def tile_moe_nxt_lin_none_kernel(tc, xT, w_words, w_scales, wp, gate, offs, out)
         gated_rows(0, 0)
         gated_rows(0, 1, True)
         turn(0)
-        group_c(first, 0)
-        group_wp(0, 1, nc.scalar.copy)
-        quantise_c(first)
+        group_c(units[0], 0)
+        group_wp(0, 1, nc.vector.tensor_copy)
+        quantise_c(units[0])
         quantise_wp(0)
-        next_projection(first, low)
-        land(first, low)
+        next_projection(units[0], low)
+        land(units[0], low)
         gather(1, 3)
-        product(1)
-        gated_rows(1, 0)
-        gated_rows(1, 1)
-        turn(1)
-        group_c(second, 1)
-        quantise_c(second)
-        next_projection(second, low)
-        land(second, low)
         group_wp(1, 0, pool_copy)
         group_wp(1, 1, nc.vector.tensor_copy)
         quantise_wp(1)
-        gather(3, E)
-        for unit in (first, second):
-            next_projection(unit, high)
-            land(unit, high)
-        for unit in (third, fourth):
+        next_projection(units[0], high)
+        land(units[0], high)
+        for i in range(1, len(units)):
+            unit = units[i]
             for e in unit:
+                if e == 3:
+                    gather(3, E)
                 product(e)
                 gated_rows(e, 0)
                 gated_rows(e, 1)
                 turn(e)
                 group_c(unit, e)
             quantise_c(unit)
-            for half in (low, high):
-                next_projection(unit, half)
-                land(unit, half)
-        for unit in (first, second, third):
+            if i > 1:
+                land(units[i - 1], high, after=unit)
+            next_projection(unit, low)
+            land(unit, low)
+            next_projection(unit, high)
+        land(units[-1], high)
+        for unit in units[:-1]:
             for f in low + high:
                 scatter(unit, f)
         for f in low + high:
-            scatter(fourth, f)
+            scatter(units[-1], f)
             nc.sync.dma_start(out=out[f * P : (f + 1) * P, :], in_=windows[f][:])

@@ -35,7 +35,6 @@ def tile_moe_nxt_lin_none_kernel(tc, xT, w_words, w_scales, wp, gate, offs, out)
     nc = tc.nc
     with ExitStack() as ctx:
         keep = ctx.enter_context(tc.tile_pool(name="keep", bufs=1))
-        ring = ctx.enter_context(tc.tile_pool(name="ring", bufs=3))
         psum_y = ctx.enter_context(tc.psum_pool(name="psum_y", bufs=4))
         psum_t = ctx.enter_context(tc.psum_pool(name="psum_t", bufs=2))
         psum_o = ctx.enter_context(tc.psum_pool(name="psum_o", bufs=2))
@@ -133,7 +132,7 @@ def tile_moe_nxt_lin_none_kernel(tc, xT, w_words, w_scales, wp, gate, offs, out)
 
         def gated_rows(e, g, on_vector=False):
             if g == 0:
-                rows[e] = ring.tile([P, N], BF16, name="c_rows", align_bytes=64)
+                rows[e] = keep.tile([P, N], BF16, name=f"c_rows{e}", tag=f"swap{e}", align_bytes=64)
             gate_times(e, g, ys[e][g], rows[e], on_vector)
 
         def turn(e):
@@ -148,7 +147,7 @@ def tile_moe_nxt_lin_none_kernel(tc, xT, w_words, w_scales, wp, gate, offs, out)
         def group_c(unit, e):
             width = len(unit) * C
             if e == unit[0]:
-                groups[unit] = keep.tile([P, PASSES, width, PACK], BF16, name=f"c_group{e}", tag=f"swap{e}", align_bytes=64)
+                groups[unit] = keep.tile([P, PASSES, width, PACK], BF16, name=f"c_group{e}", align_bytes=64)
             words = groups[unit][:].rearrange("p g s j -> p (g s j)").bitcast(F32).rearrange("p (g s u) -> p g s u", g=PASSES, u=2)
             at = (e - unit[0]) * C
             nc.scalar.copy(out=words[:, :, at : at + C, :], in_=turned_of[e][:].rearrange("p g u s -> p g s u"))
@@ -208,7 +207,7 @@ def tile_moe_nxt_lin_none_kernel(tc, xT, w_words, w_scales, wp, gate, offs, out)
         def land(unit, f_tiles, after=None):
             width = len(unit) * C
             label = f"landed{unit[0]}{f_tiles[0]}"
-            tag = f"swap{after[0]}" if after else label
+            tag = f"swap{after[-1]}" if after else label
             tile = keep.tile([P, len(f_tiles), width], F32, name=label, tag=tag, align_bytes=64)
             nc.scalar.copy(
                 out=tile[:].rearrange("p f s -> p (f s)"), in_=sums[unit, f_tiles][:, : len(f_tiles) * width]

from contextlib import ExitStack

import concourse.mybir as mybir
from concourse.masks import make_identity

K, T, E, C, N, M = 512, 768, 6, 128, 1024, 512
P = 128
PACK = 4
PASSES = N // 512
F_TILES = M // P

FLOPS = 2 * K * N * E * C + 2 * N * M * T
BYTES = 4 * K * T + E * K * N // 2 + E * (K // 32) * N + 4 * N * M + 4 * E * C + 2 * E * C + 4 * M * T

F32 = mybir.dt.float32
BF16 = mybir.dt.bfloat16
I32 = mybir.dt.int32
U32 = mybir.dt.uint32
U16 = mybir.dt.uint16
U8 = mybir.dt.uint8
FP8X4 = mybir.dt.float8_e4m3fn_x4
FP4X4 = mybir.dt.float4_e2m1fn_x4
COPY = mybir.ActivationFunctionType.Copy
MULT = mybir.AluOpType.mult


def interleave(copy, dst, src, a, b):
    copy(
        out=dst[:, PACK * a : PACK * b].rearrange("p (c i j) -> p c j i", i=4, j=PACK),
        in_=src[:, :, a:b].rearrange("p j (c i) -> p c j i", i=4),
    )


def tile_moe_nxt_lin_none_kernel(tc, xT, w_words, w_scales, wp, gate, offs, out):
    nc = tc.nc
    with ExitStack() as ctx:
        keep = ctx.enter_context(tc.tile_pool(name="keep", bufs=1))
        psum_y = ctx.enter_context(tc.psum_pool(name="psum_y", bufs=4))
        psum_t = ctx.enter_context(tc.psum_pool(name="psum_t", bufs=2))
        psum_o = ctx.enter_context(tc.psum_pool(name="psum_o", bufs=2))

        offsets = keep.tile([P, E * C // 16], U16, name="offsets")
        gate_cols = keep.tile([P, E], F32, name="gate_cols")
        gate_rows = keep.tile([P, P], F32, name="gate_rows")
        ident = keep.tile([P, P], F32, name="ident")
        x_codes = keep.tile([P, T], U32, name="x_codes", align_bytes=64)
        x_scales = keep.tile([P, T], U8, name="x_scales", align_bytes=64)
        s_codes = keep.tile([P, E * C], U32, name="s_codes", align_bytes=64)
        s_scales = keep.tile([P, E * C], U8, name="s_scales", align_bytes=64)
        w_codes = keep.tile([P, E, 2 * N], U8, name="w_codes", align_bytes=64)
        w_planes = keep.tile([P, E, N], U8, name="w_planes", align_bytes=64)

        nc.vector.memset(w_planes[:].rearrange("p e n -> p (e n)").bitcast(I32), 0)
        nc.gpsimd.memset(x_scales[:], 0)
        nc.gpsimd.memset(gate_rows[:], 0.0)
        make_identity(nc, ident[:])

        x_view = xT.rearrange("(p j) t -> p j t", j=PACK)
        x_cuts = ((0, 256), (256, 512), (512, T))
        x_raw = []
        for a, b in x_cuts:
            raw = keep.tile([P, PACK, b - a], F32, name=f"x_raw{a}")
            nc.sync.dma_start(out=raw[:], in_=x_view[:, :, a:b])
            x_raw.append(raw)
        nc.sync.dma_start(offsets[:], offs)
        nc.sync.dma_start(out=gate_rows[0:E, :], in_=gate[0:1, :].rearrange("o (e p) -> (o e) p", p=P))

        def load_w(a, b):
            nc.sync.dma_start(out=w_codes[:, a:b, :].bitcast(I32), in_=w_words[a:b, 0].rearrange("e p n -> p e n").bitcast(I32))

        wp_view = wp.rearrange("(g p j) f -> g p j f", p=P, j=PACK)
        wp_raw = {}

        def load_wp(half, g):
            raw = keep.tile([P, PACK, M // 2], F32, name=f"wp_raw{half}{g}")
            nc.sync.dma_start(out=raw[:], in_=wp_view[g, :, :, half * (M // 2) : (half + 1) * (M // 2)])
            wp_raw[half, g] = raw

        load_wp(0, 0)
        load_w(0, 1)
        scale_rows = w_scales.bitcast(I32).rearrange("e a (q r) n -> r q (e a) n", r=4)
        for r in range(4):
            nc.sync.dma_start(out=w_planes[r:P:32, :, :].bitcast(I32), in_=scale_rows[r])
        load_wp(0, 1)
        load_w(1, 3)
        load_wp(1, 0)
        load_wp(1, 1)
        load_w(3, E)

        x_group = keep.tile([P, PACK * T], BF16, name="x_group", align_bytes=64)
        for (a, b), raw in zip(x_cuts, x_raw):
            width = b - a
            dst = x_group[:, PACK * a : PACK * b]
            cut = 96
            interleave(nc.scalar.copy, dst, raw, 0, cut)
            interleave(nc.vector.tensor_copy, dst, raw, cut, width)
            nc.vector.quantize_mx(out=x_codes[:, a:b].bitcast(FP8X4), scales=x_scales[:, a:b], in_=dst)

        def gather(a, b):
            at = offsets[:, a * C // 16 : b * C // 16]
            nc.vector.tensor_copy(s_codes[:, a * C : b * C], x_codes[:].indirect(at))
            nc.vector.tensor_copy(s_scales[:, a * C : b * C], x_scales[:].indirect(at))

        def gate_times(e, g, y, c_rows, on_vector):
            dst = c_rows[:, 512 * g : 512 * (g + 1)].rearrange("s (u p i) -> s u p i", u=2, i=2)
            src = y[:].rearrange("s (p u i) -> s u p i", u=2, i=2)
            if on_vector:
                nc.vector.tensor_scalar(dst, src, gate_cols[:, e : e + 1], None, MULT)
            else:
                nc.scalar.activation(out=dst, in_=src, func=COPY, scale=gate_cols[:, e : e + 1])

        ys = {}

        def product(e):
            ys[e] = []
            for g in range(PASSES):
                y = psum_y.tile([P, 512], F32, name="y")
                nc.tensor.matmul_mx(
                    out=y[:],
                    lhsT=s_codes[:, e * C : (e + 1) * C].bitcast(FP8X4),
                    lhsT_scale=s_scales[:, e * C : (e + 1) * C],
                    rhs=w_codes[:, e, 1024 * g : 1024 * (g + 1)].bitcast(FP4X4),
                    rhs_scale=w_planes[:, e, 512 * g : 512 * (g + 1)],
                    start=True,
                    stop=True,
                )
                ys[e].append(y)

        groups = {}

        rows, turned_of, groups, c_quant, sums, landed = {}, {}, {}, {}, {}, {}

        def gated_rows(e, g, on_vector=False):
            if g == 0:
                rows[e] = keep.tile([P, N], BF16, name=f"c_rows{e}", tag=f"swap{e}", align_bytes=64)
            gate_times(e, g, ys[e][g], rows[e], on_vector)

        def turn(e):
            turned = psum_t.tile([P, PASSES, 2, C], F32, name="turned")
            words = rows[e][:].bitcast(F32)
            for g in range(PASSES):
                for u in range(2):
                    at = 256 * g + 128 * u
                    nc.tensor.transpose(turned[:, g, u, :], words[:, at : at + 128], ident[:])
            turned_of[e] = turned

        def group_c(unit, e):
            width = len(unit) * C
            if e == unit[0]:
                groups[unit] = keep.tile([P, PASSES, width, PACK], BF16, name=f"c_group{e}", align_bytes=64)
            words = groups[unit][:].rearrange("p g s j -> p (g s j)").bitcast(F32).rearrange("p (g s u) -> p g s u", g=PASSES, u=2)
            at = (e - unit[0]) * C
            nc.scalar.copy(out=words[:, :, at : at + C, :], in_=turned_of[e][:].rearrange("p g u s -> p g s u"))

        def quantise_c(unit):
            width = len(unit) * C
            codes = keep.tile([P, PASSES, width], U32, name=f"c_codes{unit[0]}", align_bytes=64)
            scales = keep.tile([P, PASSES, width], U8, name=f"c_scales{unit[0]}", align_bytes=64)
            nc.vector.quantize_mx(
                out=codes[:].rearrange("p g s -> p (g s)").bitcast(FP8X4),
                scales=scales[:].rearrange("p g s -> p (g s)"),
                in_=groups[unit][:].rearrange("p g s j -> p (g s j)"),
            )
            c_quant[unit] = (codes, scales)

        half_width = M // 2
        wp_codes, wp_scales, wp_group = [], [], []
        for half in range(2):
            wp_group.append(keep.tile([P, PASSES * half_width * PACK], BF16, name=f"wp_group{half}", align_bytes=64))
            wp_codes.append(keep.tile([P, PASSES, half_width], U32, name=f"wp_codes{half}", align_bytes=64))
            wp_scales.append(keep.tile([P, PASSES, half_width], U8, name=f"wp_scales{half}", align_bytes=64))

        def pool_copy(out, in_):
            nc.gpsimd.tensor_scalar(out, in_, 1.0, 0.0, MULT, mybir.AluOpType.add)

        def group_wp(half, g, copy):
            dst = wp_group[half][:, PACK * half_width * g : PACK * half_width * (g + 1)]
            interleave(copy, dst, wp_raw[half, g], 0, half_width)

        def quantise_wp(half):
            nc.vector.quantize_mx(
                out=wp_codes[half][:].rearrange("p g f -> p (g f)").bitcast(FP8X4),
                scales=wp_scales[half][:].rearrange("p g f -> p (g f)"),
                in_=wp_group[half][:],
            )

        windows = [keep.tile([P, T], F32, name=f"window{f}") for f in range(F_TILES)]

        def next_projection(unit, f_tiles):
            width = len(unit) * C
            o = psum_o.tile([P, 512], F32, name="o")
            codes, scales = c_quant[unit]
            for i, f in enumerate(f_tiles):
                half, at = f // 2, (f % 2) * P
                for g in range(PASSES):
                    nc.tensor.matmul_mx(
                        out=o[:, i * width : (i + 1) * width],
                        lhsT=wp_codes[half][:, g, at : at + P].bitcast(FP8X4),
                        lhsT_scale=wp_scales[half][:, g, at : at + P],
                        rhs=codes[:, g, :].bitcast(FP8X4),
                        rhs_scale=scales[:, g, :],
                        start=(g == 0),
                        stop=(g == PASSES - 1),
                    )
            sums[unit, f_tiles] = o

        def land(unit, f_tiles, after=None):
            width = len(unit) * C
            label = f"landed{unit[0]}{f_tiles[0]}"
            tag = f"swap{after[-1]}" if after else label
            tile = keep.tile([P, len(f_tiles), width], F32, name=label, tag=tag, align_bytes=64)
            nc.scalar.copy(
                out=tile[:].rearrange("p f s -> p (f s)"), in_=sums[unit, f_tiles][:, : len(f_tiles) * width]
            )
            for i, f in enumerate(f_tiles):
                landed[unit, f] = tile[:, i, :]

        def scatter(unit, f):
            a, b = unit[0], unit[-1] + 1
            nc.vector.tensor_copy(windows[f][:].indirect(offsets[:, a * C // 16 : b * C // 16]), landed[unit, f])

        low, high = (0, 1), (2, 3)
        units = ((0,), (1,), (2,), (3, 4), (5,))

        gather(0, 1)
        turned = psum_t.tile([P, PASSES, 2, C], F32, name="turned")
        nc.tensor.transpose(turned[:, 0, 0, :], gate_rows[:], ident[:])
        nc.vector.tensor_copy(out=gate_cols[:], in_=turned[:, 0, 0, 0:E])
        product(0)
        group_wp(0, 0, nc.scalar.copy)
        gated_rows(0, 0)
        gated_rows(0, 1, True)
        turn(0)
        group_c(units[0], 0)
        group_wp(0, 1, nc.vector.tensor_copy)
        quantise_c(units[0])
        quantise_wp(0)
        next_projection(units[0], low)
        land(units[0], low)
        gather(1, 3)
        group_wp(1, 0, pool_copy)
        group_wp(1, 1, nc.vector.tensor_copy)
        quantise_wp(1)
        next_projection(units[0], high)
        land(units[0], high)
        for i in range(1, len(units)):
            unit = units[i]
            for e in unit:
                if e == 3:
                    gather(3, E)
                product(e)
                gated_rows(e, 0)
                gated_rows(e, 1)
                turn(e)
                group_c(unit, e)
            quantise_c(unit)
            if i > 1:
                land(units[i - 1], high, after=unit)
            next_projection(unit, low)
            land(unit, low)
            next_projection(unit, high)
        land(units[-1], high)
        for unit in units[:-1]:
            for f in low + high:
                scatter(unit, f)
        for f in low + high:
            scatter(units[-1], f)
            nc.sync.dma_start(out=out[f * P : (f + 1) * P, :], in_=windows[f][:])
